import numpy as np
import ml_dtypes


def mxq(x, axis, fmt="e4m3"):
    dtype, down = {"e4m3": (ml_dtypes.float8_e4m3fn, 7), "e5m2": (ml_dtypes.float8_e5m2, 14)}[fmt]
    v = np.moveaxis(np.asarray(x, np.float32).astype(ml_dtypes.bfloat16).astype(np.float64), axis, -1)
    blocks = v.reshape(v.shape[:-1] + (-1, 32))
    amax = np.abs(blocks).max(-1, keepdims=True)
    byte = np.maximum(np.where(amax > 0, np.frexp(amax)[1] - 1 + 127, 0) - down, 1)
    scale = np.exp2(byte - 127.0)
    codes = (blocks / scale).astype(np.float32).astype(dtype).astype(np.float64)
    return np.moveaxis((codes * scale).reshape(v.shape), -1, axis)


WIDE = False


def mx_kscale(k):
    if not WIDE:
        return np.ones(k)
    levels = np.array([10, -10, 5, -5, 0])
    if k % 512:
        return np.exp2(np.random.permutation(np.resize(levels, k // 32))).repeat(32)
    a = np.empty((k // 512, 16))
    for p in range(k // 512):
        a[p, :8] = np.random.permutation(np.resize(levels, 8))
        for g in range(8):
            far = levels[np.abs(levels - a[p, g]) >= 10]
            a[p, g + 8] = far[np.random.randint(len(far))]
    return np.exp2(a.ravel()).repeat(32)


def f64(x):
    return np.asarray(x).astype(np.float64)


def striped(idx):
    return np.tile(idx.reshape(-1, 16).T, (8, 1)).astype(np.uint16)


def unstriped(offs):
    return offs[:16].T.reshape(-1).astype(np.int64)


def relu(v):
    return np.maximum(v, 0.0)


K, T, E, C, H, N = 1024, 2048, 8, 128, 512, 128


def by_expert(wq, xq):
    return np.concatenate([wq[e].T @ xq[:, e * C:(e + 1) * C] for e in range(E)], axis=1)


def setup_inputs():
    n = np.random.standard_normal
    s = mx_kscale(K)[:, None]
    u = mx_kscale(H)
    return {
        "xT": (n((K, T)) * s).astype(np.float32),
        "w1": (n((E, K, H)) / np.sqrt(K) / s[None] * u[None, None, :]).astype(np.float32),
        "w2": (n((E, H, N)) / np.sqrt(H) / u[None, :, None]).astype(np.float32),
        "gate": np.tile(np.random.uniform(0.2, 1.0, E * C), (N, 1)).astype(np.float32),
        "offs": striped(np.random.permutation(T)[:E * C]),
    }


def reference(xT, w1, w2, gate, offs):
    idx = unstriped(offs)
    xq = mxq(f64(xT)[:, idx], 0, "e4m3")
    h = relu(by_expert(mxq(f64(w1), 1, "e4m3"), xq))
    y = by_expert(mxq(f64(w2), 1, "e4m3"), mxq(h, 0, "e4m3"))
    out = np.zeros((N, T))
    out[:, idx] = f64(gate) * y
    return out

@@ -1,0 +1,255 @@
+from contextlib import ExitStack
+
+import concourse.mybir as mybir
+
+K, T, E, C, H, N = 1024, 2048, 8, 128, 512, 128
+FLOPS = 2 * E * C * (K * H + H * N)
+
+F32 = mybir.dt.float32
+BF16 = mybir.dt.bfloat16
+U32 = mybir.dt.uint32
+U16 = mybir.dt.uint16
+U8 = mybir.dt.uint8
+FP8X4 = mybir.dt.float8_e4m3fn_x4
+RELU = mybir.ActivationFunctionType.Relu
+MULT = mybir.AluOpType.mult
+ADD = mybir.AluOpType.add
+
+P = 128
+PASSES = K // 512
+HALF = 512
+S_TOK = 1024
+W1_COLS = PASSES * 4 * H
+W2_AT = W1_COLS
+GATE_AT = W2_AT + 4 * N
+RAW_COLS = GATE_AT + 2 * C
+AHEAD = 5
+LAST_CUT = (64, 80)
+
+
+def tile_routed_moe_kernel(tc, xT, w1, w2, gate, offs, out):
+    nc = tc.nc
+    with ExitStack() as ctx:
+        keep = ctx.enter_context(tc.tile_pool(name="keep", bufs=1))
+        rawp = ctx.enter_context(tc.tile_pool(name="rawp", bufs=AHEAD))
+        grpp = ctx.enter_context(tc.tile_pool(name="grpp", bufs=4))
+        w1cp = ctx.enter_context(tc.tile_pool(name="w1cp", bufs=4))
+        hp = ctx.enter_context(tc.tile_pool(name="hp", bufs=3))
+        yp = ctx.enter_context(tc.tile_pool(name="yp", bufs=2))
+        aps = ctx.enter_context(tc.psum_pool(name="aps", bufs=3))
+        yps = ctx.enter_context(tc.psum_pool(name="yps", bufs=2))
+
+        offs_t = keep.tile([P, E * C // 16], U16, name="offs_t")
+        nc.sync.dma_start(offs_t[:], offs)
+
+        window = keep.tile([P, T], F32, name="window")
+        nc.vector.memset(window[:], 0.0)
+
+        warm = keep.tile([P, 8], F32, name="warm")
+        nc.gpsimd.memset(warm[:], 0.0)
+        warm2 = keep.tile([P, 8], F32, name="warm2")
+        nc.scalar.activation(out=warm2[:], in_=warm[:], func=RELU)
+
+        wraw = {}
+
+        def load_w2(tile_ap, at, e):
+            nc.sync.dma_start(
+                out=tile_ap[:, at : at + 4 * N],
+                in_=w2[e].rearrange("(p j) n -> p (j n)", j=4),
+            )
+
+        def load_gate(tile_ap, at, pr):
+            nc.sync.dma_start(
+                out=tile_ap[:, at : at + 2 * C],
+                in_=gate[:, 2 * C * pr : 2 * C * (pr + 1)],
+            )
+
+        def load_step(s):
+            wr = rawp.tile([P, RAW_COLS], F32, name="raw")
+            if s < E:
+                for g in range(PASSES):
+                    nc.sync.dma_start(
+                        out=wr[:, 4 * H * g : 4 * H * (g + 1)],
+                        in_=w1[s, 512 * g : 512 * (g + 1), :].rearrange("(p j) c -> p (j c)", j=4),
+                    )
+            if s >= 1:
+                load_w2(wr, W2_AT, s - 1)
+            if s >= 3 and s % 2 == 1:
+                load_gate(wr, GATE_AT, (s - 3) // 2)
+            if s == E:
+                load_gate(wr, GATE_AT, E // 2 - 1)
+            wraw[s] = wr
+
+        grouped = {}
+
+        def weights_pass(s, g):
+            wr = wraw[s]
+            if g == 0:
+                gq = grpp.tile([P, PASSES, 4 * H], BF16, name="gq", align_bytes=64)
+                w1c = w1cp.tile([P, PASSES, H], U32, name="w1c", align_bytes=64)
+                w1s = w1cp.tile([P, PASSES, H], U8, name="w1s", align_bytes=64)
+                grouped[s] = (gq, w1c, w1s)
+            gq, w1c, w1s = grouped[s]
+            last = s == E - 1
+            dst = gq[:, g, :].rearrange("p (t m j) -> p m j t", t=4, m=P, j=4)
+            src = wr[:, 4 * H * g : 4 * H * (g + 1)].rearrange("p (j m t) -> p m j t", j=4, t=4)
+            if last:
+                cut = LAST_CUT[g]
+                nc.vector.tensor_copy(out=dst[:, 0:cut], in_=src[:, 0:cut])
+                nc.scalar.copy(out=dst[:, cut:P], in_=src[:, cut:P])
+                nc.vector.quantize_mx(
+                    out=w1c[:, g, :].bitcast(FP8X4), scales=w1s[:, g, :], in_=gq[:, g, :]
+                )
+            elif g == 0:
+                nc.scalar.copy(out=dst, in_=src)
+            else:
+                nc.vector.tensor_copy(out=dst, in_=src)
+            if g == 0:
+                return
+            if not last:
+                nc.vector.quantize_mx(
+                    out=w1c[:].rearrange("p g c -> p (g c)").bitcast(FP8X4),
+                    scales=w1s[:].rearrange("p g c -> p (g c)"),
+                    in_=gq[:].rearrange("p g c -> p (g c)"),
+                )
+            codes[s] = (w1c, w1s)
+
+        load_step(0)
+
+        x_view = xT.rearrange("(g p u e) n -> g u p (e n)", g=PASSES, p=P, u=2, e=2)
+        xraw = {}
+        for g in range(PASSES):
+            for u in range(2):
+                xr = rawp.tile([P, RAW_COLS], F32, name="raw")
+                nc.sync.dma_start(out=xr[:, 0 : 2 * T], in_=x_view[g, u])
+                xraw[(g, u)] = xr
+
+        codes = {}
+        weights_pass(0, 0)
+        weights_pass(0, 1)
+
+        pairs = {}
+        for g in range(PASSES):
+            for u in range(2):
+                pt = keep.tile([P, T, 2], BF16, name="pairs%d%d" % (g, u))
+                xr = xraw[(g, u)][:, 0 : 2 * T].rearrange("p (e n) -> p e n", e=2)
+                nc.scalar.copy(
+                    out=pt[:, 0:S_TOK, :].rearrange("p (c i) e -> p c e i", i=4),
+                    in_=xr[:, :, 0:S_TOK].rearrange("p e (c i) -> p c e i", i=4),
+                )
+                nc.gpsimd.tensor_scalar(
+                    out=pt[:, S_TOK:T, :],
+                    in0=xr[:, :, S_TOK:T].rearrange("p e n -> p n e"),
+                    scalar1=1.0,
+                    scalar2=0.0,
+                    op0=MULT,
+                    op1=ADD,
+                )
+                pairs[(g, u)] = pt
+
+        for s in range(1, AHEAD + 1):
+            load_step(s)
+
+        xc = {}
+        xs = {}
+
+        def tokens(hf):
+            xg = keep.tile([P, PASSES, HALF, 4], BF16, name="xg%d" % hf, align_bytes=64)
+            for g in range(PASSES):
+                words = xg[:, g].rearrange("p n t -> p (n t)").bitcast(U32)
+                words = words.rearrange("p (n u) -> p n u", u=2)
+                for u in range(2):
+                    win = pairs[(g, u)][:].rearrange("p n e -> p (n e)").bitcast(U32)
+                    nc.vector.tensor_copy(
+                        out=words[:, :, u],
+                        in_=win.indirect(offs_t[:, 32 * hf : 32 * (hf + 1)]),
+                    )
+            xch = keep.tile([P, PASSES, HALF], U32, name="xc%d" % hf, align_bytes=64)
+            xsh = keep.tile([P, PASSES, HALF], U8, name="xs%d" % hf, align_bytes=64)
+            nc.vector.quantize_mx(
+                out=xch[:].rearrange("p g n -> p (g n)").bitcast(FP8X4),
+                scales=xsh[:].rearrange("p g n -> p (g n)"),
+                in_=xg[:].rearrange("p g n t -> p (g n t)"),
+            )
+            xc[hf] = xch
+            xs[hf] = xsh
+
+        a_tiles = {}
+        y_tiles = {}
+
+        def layer1(s):
+            w1c, w1s = codes[s]
+            order = (1, 0) if s == E - 1 else (0, 1)
+            cols = slice(C * (s % 4), C * (s % 4 + 1))
+            a_ps = aps.tile([P, 4, C], F32, name="a_ps")
+            for t in range(4):
+                for g in order:
+                    nc.tensor.matmul_mx(
+                        out=a_ps[:, t, :],
+                        lhsT=w1c[:, g, P * t : P * (t + 1)].bitcast(FP8X4),
+                        lhsT_scale=w1s[:, g, P * t : P * (t + 1)],
+                        rhs=xc[s // 4][:, g, cols].bitcast(FP8X4),
+                        rhs_scale=xs[s // 4][:, g, cols],
+                        start=(g == order[0]),
+                        stop=(g == order[1]),
+                    )
+            a_tiles[s] = a_ps
+
+        def layer2(e):
+            hw = hp.tile([P, 2 * 4 * C], BF16, name="hw", align_bytes=64)
+            nc.scalar.activation(
+                out=hw[:, 0 : 4 * C].rearrange("p (c t) -> p c t", t=4),
+                in_=a_tiles[e][:].rearrange("p t c -> p c t"),
+                func=RELU,
+            )
+            nc.scalar.copy(
+                out=hw[:, 4 * C : 8 * C].rearrange("p (c i j) -> p c j i", i=4, j=4),
+                in_=wraw[e + 1][:, W2_AT : W2_AT + 4 * N].rearrange("p (j c i) -> p c j i", j=4, i=4),
+            )
+            hwc = hp.tile([P, 2 * C], U32, name="hwc", align_bytes=64)
+            hws = hp.tile([P, 2 * C], U8, name="hws", align_bytes=64)
+            nc.vector.quantize_mx(out=hwc[:].bitcast(FP8X4), scales=hws[:], in_=hw[:])
+            if e % 2 == 0:
+                y_ps = yps.tile([P, 2, C], F32, name="y_ps")
+                y_tiles[e // 2] = y_ps
+            nc.tensor.matmul_mx(
+                out=y_tiles[e // 2][:, e % 2, :],
+                lhsT=hwc[:, C : 2 * C].bitcast(FP8X4),
+                lhsT_scale=hws[:, C : 2 * C],
+                rhs=hwc[:, 0:C].bitcast(FP8X4),
+                rhs_scale=hws[:, 0:C],
+                start=True,
+                stop=True,
+            )
+
+        def way_back(pr, gate_tile):
+            y_sb = yp.tile([P, 2 * C], F32, name="y_sb")
+            nc.scalar.copy(out=y_sb[:], in_=y_tiles[pr][:].rearrange("p e c -> p (e c)"))
+            nc.vector.tensor_tensor(
+                out=window[:].indirect(offs_t[:, 16 * pr : 16 * (pr + 1)]),
+                in0=y_sb[:],
+                in1=gate_tile[:, GATE_AT : GATE_AT + 2 * C],
+                op=MULT,
+            )
+
+        weights_pass(1, 0)
+        tokens(0)
+        for s in range(E + 1):
+            if s + 2 <= E - 1:
+                weights_pass(s + 2, 0)
+            if 1 <= s < E:
+                weights_pass(s, 1)
+            if s < E:
+                layer1(s)
+            if s >= 1:
+                layer2(s - 1)
+            if s == 1:
+                tokens(1)
+            if s >= 3 and s % 2 == 1:
+                way_back((s - 3) // 2, wraw[s])
+            if s == E:
+                way_back(E // 2 - 1, wraw[s])
+            if s >= 1 and s + AHEAD <= E:
+                load_step(s + AHEAD)
+
+        nc.sync.dma_start(out=out, in_=window[:])

@@ -224,12 +224,15 @@ def tile_routed_moe_kernel(tc, xT, w1, w2, gate, offs, out):
 
         def way_back(pr, gate_tile):
             y_sb = yp.tile([P, 2 * C], F32, name="y_sb")
-            nc.scalar.copy(out=y_sb[:], in_=y_tiles[pr][:].rearrange("p e c -> p (e c)"))
             nc.vector.tensor_tensor(
-                out=window[:].indirect(offs_t[:, 16 * pr : 16 * (pr + 1)]),
-                in0=y_sb[:],
+                out=y_sb[:],
+                in0=y_tiles[pr][:].rearrange("p e c -> p (e c)"),
                 in1=gate_tile[:, GATE_AT : GATE_AT + 2 * C],
                 op=MULT,
+            )
+            nc.vector.tensor_copy(
+                out=window[:].indirect(offs_t[:, 16 * pr : 16 * (pr + 1)]),
+                in_=y_sb[:],
             )
 
         weights_pass(1, 0)

@@ -17,7 +17,6 @@ ADD = mybir.AluOpType.add
 
 P = 128
 PASSES = K // 512
-HALF = 512
 S_TOK = 1024
 W1_COLS = PASSES * 4 * H
 W2_AT = W1_COLS
@@ -153,26 +152,22 @@ def tile_routed_moe_kernel(tc, xT, w1, w2, gate, offs, out):
         xc = {}
         xs = {}
 
-        def tokens(hf):
-            xg = keep.tile([P, PASSES, HALF, 4], BF16, name="xg%d" % hf, align_bytes=64)
-            for g in range(PASSES):
-                words = xg[:, g].rearrange("p n t -> p (n t)").bitcast(U32)
-                words = words.rearrange("p (n u) -> p n u", u=2)
-                for u in range(2):
-                    win = pairs[(g, u)][:].rearrange("p n e -> p (n e)").bitcast(U32)
-                    nc.vector.tensor_copy(
-                        out=words[:, :, u],
-                        in_=win.indirect(offs_t[:, 32 * hf : 32 * (hf + 1)]),
-                    )
-            xch = keep.tile([P, PASSES, HALF], U32, name="xc%d" % hf, align_bytes=64)
-            xsh = keep.tile([P, PASSES, HALF], U8, name="xs%d" % hf, align_bytes=64)
+        def tokens(g):
+            xg = keep.tile([P, E * C, 4], BF16, name="xg%d" % g, align_bytes=64)
+            words = xg[:].rearrange("p n t -> p (n t)").bitcast(U32)
+            words = words.rearrange("p (n u) -> p n u", u=2)
+            for u in range(2):
+                win = pairs[(g, u)][:].rearrange("p n e -> p (n e)").bitcast(U32)
+                nc.vector.tensor_copy(out=words[:, :, u], in_=win.indirect(offs_t[:]))
+            xcg = keep.tile([P, E * C], U32, name="xc%d" % g, align_bytes=64)
+            xsg = keep.tile([P, E * C], U8, name="xs%d" % g, align_bytes=64)
             nc.vector.quantize_mx(
-                out=xch[:].rearrange("p g n -> p (g n)").bitcast(FP8X4),
-                scales=xsh[:].rearrange("p g n -> p (g n)"),
-                in_=xg[:].rearrange("p g n t -> p (g n t)"),
+                out=xcg[:].bitcast(FP8X4),
+                scales=xsg[:],
+                in_=xg[:].rearrange("p n t -> p (n t)"),
             )
-            xc[hf] = xch
-            xs[hf] = xsh
+            xc[g] = xcg
+            xs[g] = xsg
 
         a_tiles = {}
         y_tiles = {}
@@ -180,7 +175,7 @@ def tile_routed_moe_kernel(tc, xT, w1, w2, gate, offs, out):
         def layer1(s):
             w1c, w1s = codes[s]
             order = (1, 0) if s == E - 1 else (0, 1)
-            cols = slice(C * (s % 4), C * (s % 4 + 1))
+            cols = slice(C * s, C * (s + 1))
             a_ps = aps.tile([P, 4, C], F32, name="a_ps")
             for t in range(4):
                 for g in order:
@@ -188,8 +183,8 @@ def tile_routed_moe_kernel(tc, xT, w1, w2, gate, offs, out):
                         out=a_ps[:, t, :],
                         lhsT=w1c[:, g, P * t : P * (t + 1)].bitcast(FP8X4),
                         lhsT_scale=w1s[:, g, P * t : P * (t + 1)],
-                        rhs=xc[s // 4][:, g, cols].bitcast(FP8X4),
-                        rhs_scale=xs[s // 4][:, g, cols],
+                        rhs=xc[g][:, cols].bitcast(FP8X4),
+                        rhs_scale=xs[g][:, cols],
                         start=(g == order[0]),
                         stop=(g == order[1]),
                     )
@@ -237,6 +232,7 @@ def tile_routed_moe_kernel(tc, xT, w1, w2, gate, offs, out):
 
         weights_pass(1, 0)
         tokens(0)
+        tokens(1)
         for s in range(E + 1):
             if s + 2 <= E - 1:
                 weights_pass(s + 2, 0)
@@ -246,8 +242,6 @@ def tile_routed_moe_kernel(tc, xT, w1, w2, gate, offs, out):
                 layer1(s)
             if s >= 1:
                 layer2(s - 1)
-            if s == 1:
-                tokens(1)
             if s >= 3 and s % 2 == 1:
                 way_back((s - 3) // 2, wraw[s])
             if s == E:

@@ -94,11 +94,16 @@ def tile_routed_moe_kernel(tc, xT, w1, w2, gate, offs, out):
             src = wr[:, 4 * H * g : 4 * H * (g + 1)].rearrange("p (j m t) -> p m j t", j=4, t=4)
             if last:
                 cut = LAST_CUT[g]
+                if g == 1:
+                    nc.vector.quantize_mx(
+                        out=w1c[:, 0, :].bitcast(FP8X4), scales=w1s[:, 0, :], in_=gq[:, 0, :]
+                    )
                 nc.vector.tensor_copy(out=dst[:, 0:cut], in_=src[:, 0:cut])
                 nc.scalar.copy(out=dst[:, cut:P], in_=src[:, cut:P])
-                nc.vector.quantize_mx(
-                    out=w1c[:, g, :].bitcast(FP8X4), scales=w1s[:, g, :], in_=gq[:, g, :]
-                )
+                if g == 1:
+                    nc.vector.quantize_mx(
+                        out=w1c[:, 1, :].bitcast(FP8X4), scales=w1s[:, 1, :], in_=gq[:, 1, :]
+                    )
             elif g == 0:
                 nc.scalar.copy(out=dst, in_=src)
             else:

@@ -23,7 +23,7 @@ W2_AT = W1_COLS
 GATE_AT = W2_AT + 4 * N
 RAW_COLS = GATE_AT + 2 * C
 AHEAD = 5
-LAST_CUT = (64, 80)
+LAST_CUT = 64
 
 
 def tile_routed_moe_kernel(tc, xT, w1, w2, gate, offs, out):
@@ -92,17 +92,21 @@ def tile_routed_moe_kernel(tc, xT, w1, w2, gate, offs, out):
             last = s == E - 1
             dst = gq[:, g, :].rearrange("p (t m j) -> p m j t", t=4, m=P, j=4)
             src = wr[:, 4 * H * g : 4 * H * (g + 1)].rearrange("p (j m t) -> p m j t", j=4, t=4)
-            if last:
-                cut = LAST_CUT[g]
-                if g == 1:
-                    nc.vector.quantize_mx(
-                        out=w1c[:, 0, :].bitcast(FP8X4), scales=w1s[:, 0, :], in_=gq[:, 0, :]
-                    )
+            if last and g == 0:
+                cut = LAST_CUT
                 nc.vector.tensor_copy(out=dst[:, 0:cut], in_=src[:, 0:cut])
                 nc.scalar.copy(out=dst[:, cut:P], in_=src[:, cut:P])
-                if g == 1:
+            elif last:
+                nc.vector.quantize_mx(
+                    out=w1c[:, 0, :].bitcast(FP8X4), scales=w1s[:, 0, :], in_=gq[:, 0, :]
+                )
+                nc.vector.tensor_copy(out=dst[:, :, :, 0:2], in_=src[:, :, :, 0:2])
+                nc.scalar.copy(out=dst[:, :, :, 2:4], in_=src[:, :, :, 2:4])
+                for half in range(2):
                     nc.vector.quantize_mx(
-                        out=w1c[:, 1, :].bitcast(FP8X4), scales=w1s[:, 1, :], in_=gq[:, 1, :]
+                        out=w1c[:, 1, 2 * P * half : 2 * P * (half + 1)].bitcast(FP8X4),
+                        scales=w1s[:, 1, 2 * P * half : 2 * P * (half + 1)],
+                        in_=gq[:, 1, 2 * H * half : 2 * H * (half + 1)],
                     )
             elif g == 0:
                 nc.scalar.copy(out=dst, in_=src)

@@ -183,19 +183,18 @@ def tile_routed_moe_kernel(tc, xT, w1, w2, gate, offs, out):
 
         def layer1(s):
             w1c, w1s = codes[s]
-            order = (1, 0) if s == E - 1 else (0, 1)
             cols = slice(C * s, C * (s + 1))
             a_ps = aps.tile([P, 4, C], F32, name="a_ps")
             for t in range(4):
-                for g in order:
+                for g in range(PASSES):
                     nc.tensor.matmul_mx(
                         out=a_ps[:, t, :],
                         lhsT=w1c[:, g, P * t : P * (t + 1)].bitcast(FP8X4),
                         lhsT_scale=w1s[:, g, P * t : P * (t + 1)],
                         rhs=xc[g][:, cols].bitcast(FP8X4),
                         rhs_scale=xs[g][:, cols],
-                        start=(g == order[0]),
-                        stop=(g == order[1]),
+                        start=(g == 0),
+                        stop=(g == PASSES - 1),
                     )
             a_tiles[s] = a_ps
 

@@ -23,6 +23,7 @@ W2_AT = W1_COLS
 GATE_AT = W2_AT + 4 * N
 RAW_COLS = GATE_AT + 2 * C
 AHEAD = 5
+PASS0_CUT = 96
 LAST_CUT = 64
 
 
@@ -109,8 +110,11 @@ def tile_routed_moe_kernel(tc, xT, w1, w2, gate, offs, out):
                         in_=gq[:, 1, 2 * H * half : 2 * H * (half + 1)],
                     )
             elif g == 0:
-                nc.scalar.copy(out=dst, in_=src)
+                nc.scalar.copy(out=dst[:, 0:PASS0_CUT], in_=src[:, 0:PASS0_CUT])
             else:
+                dst0 = gq[:, 0, :].rearrange("p (t m j) -> p m j t", t=4, m=P, j=4)
+                src0 = wr[:, 0 : 4 * H].rearrange("p (j m t) -> p m j t", j=4, t=4)
+                nc.vector.tensor_copy(out=dst0[:, PASS0_CUT:P], in_=src0[:, PASS0_CUT:P])
                 nc.vector.tensor_copy(out=dst, in_=src)
             if g == 0:
                 return

@@ -38,6 +38,7 @@ def tile_routed_moe_kernel(tc, xT, w1, w2, gate, offs, out):
         yp = ctx.enter_context(tc.tile_pool(name="yp", bufs=2))
         aps = ctx.enter_context(tc.psum_pool(name="aps", bufs=3))
         yps = ctx.enter_context(tc.psum_pool(name="yps", bufs=2))
+        lps = ctx.enter_context(tc.psum_pool(name="lps", bufs=2))
 
         offs_t = keep.tile([P, E * C // 16], U16, name="offs_t")
         nc.sync.dma_start(offs_t[:], offs)
@@ -188,11 +189,15 @@ def tile_routed_moe_kernel(tc, xT, w1, w2, gate, offs, out):
         def layer1(s):
             w1c, w1s = codes[s]
             cols = slice(C * s, C * (s + 1))
-            a_ps = aps.tile([P, 4, C], F32, name="a_ps")
+            if s == E - 1:
+                banks = [lps.tile([P, 2, C], F32, name="a_half") for half in range(2)]
+            else:
+                a_ps = aps.tile([P, 4, C], F32, name="a_ps")
+                banks = [a_ps[:, 0:2, :], a_ps[:, 2:4, :]]
             for t in range(4):
                 for g in range(PASSES):
                     nc.tensor.matmul_mx(
-                        out=a_ps[:, t, :],
+                        out=banks[t // 2][:, t % 2, :],
                         lhsT=w1c[:, g, P * t : P * (t + 1)].bitcast(FP8X4),
                         lhsT_scale=w1s[:, g, P * t : P * (t + 1)],
                         rhs=xc[g][:, cols].bitcast(FP8X4),
@@ -200,15 +205,24 @@ def tile_routed_moe_kernel(tc, xT, w1, w2, gate, offs, out):
                         start=(g == 0),
                         stop=(g == PASSES - 1),
                     )
-            a_tiles[s] = a_ps
+            a_tiles[s] = banks if s == E - 1 else a_ps
 
         def layer2(e):
             hw = hp.tile([P, 2 * 4 * C], BF16, name="hw", align_bytes=64)
-            nc.scalar.activation(
-                out=hw[:, 0 : 4 * C].rearrange("p (c t) -> p c t", t=4),
-                in_=a_tiles[e][:].rearrange("p t c -> p c t"),
-                func=RELU,
-            )
+            h_view = hw[:, 0 : 4 * C].rearrange("p (c t) -> p c t", t=4)
+            if e == E - 1:
+                for half in range(2):
+                    nc.scalar.activation(
+                        out=h_view[:, :, 2 * half : 2 * half + 2],
+                        in_=a_tiles[e][half][:].rearrange("p t c -> p c t"),
+                        func=RELU,
+                    )
+            else:
+                nc.scalar.activation(
+                    out=h_view,
+                    in_=a_tiles[e][:].rearrange("p t c -> p c t"),
+                    func=RELU,
+                )
             nc.scalar.copy(
                 out=hw[:, 4 * C : 8 * C].rearrange("p (c i j) -> p c j i", i=4, j=4),
                 in_=wraw[e + 1][:, W2_AT : W2_AT + 4 * N].rearrange("p (j c i) -> p c j i", j=4, i=4),

from contextlib import ExitStack

import concourse.mybir as mybir

K, T, E, C, H, N = 1024, 2048, 8, 128, 512, 128
FLOPS = 2 * E * C * (K * H + H * N)

F32 = mybir.dt.float32
BF16 = mybir.dt.bfloat16
U32 = mybir.dt.uint32
U16 = mybir.dt.uint16
U8 = mybir.dt.uint8
FP8X4 = mybir.dt.float8_e4m3fn_x4
RELU = mybir.ActivationFunctionType.Relu
MULT = mybir.AluOpType.mult
ADD = mybir.AluOpType.add

P = 128
PASSES = K // 512
S_TOK = 1024
W1_COLS = PASSES * 4 * H
W2_AT = W1_COLS
GATE_AT = W2_AT + 4 * N
RAW_COLS = GATE_AT + 2 * C
AHEAD = 5
PASS0_CUT = 96
LAST_CUT = 64


def tile_routed_moe_kernel(tc, xT, w1, w2, gate, offs, out):
    nc = tc.nc
    with ExitStack() as ctx:
        keep = ctx.enter_context(tc.tile_pool(name="keep", bufs=1))
        rawp = ctx.enter_context(tc.tile_pool(name="rawp", bufs=AHEAD))
        grpp = ctx.enter_context(tc.tile_pool(name="grpp", bufs=4))
        w1cp = ctx.enter_context(tc.tile_pool(name="w1cp", bufs=4))
        hp = ctx.enter_context(tc.tile_pool(name="hp", bufs=3))
        yp = ctx.enter_context(tc.tile_pool(name="yp", bufs=2))
        aps = ctx.enter_context(tc.psum_pool(name="aps", bufs=3))
        yps = ctx.enter_context(tc.psum_pool(name="yps", bufs=2))
        lps = ctx.enter_context(tc.psum_pool(name="lps", bufs=2))

        offs_t = keep.tile([P, E * C // 16], U16, name="offs_t")
        nc.sync.dma_start(offs_t[:], offs)

        window = keep.tile([P, T], F32, name="window")
        nc.vector.memset(window[:], 0.0)

        warm = keep.tile([P, 8], F32, name="warm")
        nc.gpsimd.memset(warm[:], 0.0)
        warm2 = keep.tile([P, 8], F32, name="warm2")
        nc.scalar.activation(out=warm2[:], in_=warm[:], func=RELU)

        wraw = {}

        def load_w2(tile_ap, at, e):
            nc.sync.dma_start(
                out=tile_ap[:, at : at + 4 * N],
                in_=w2[e].rearrange("(p j) n -> p (j n)", j=4),
            )

        def load_gate(tile_ap, at, pr):
            nc.sync.dma_start(
                out=tile_ap[:, at : at + 2 * C],
                in_=gate[:, 2 * C * pr : 2 * C * (pr + 1)],
            )

        def load_step(s):
            wr = rawp.tile([P, RAW_COLS], F32, name="raw")
            if s < E:
                for g in range(PASSES):
                    nc.sync.dma_start(
                        out=wr[:, 4 * H * g : 4 * H * (g + 1)],
                        in_=w1[s, 512 * g : 512 * (g + 1), :].rearrange("(p j) c -> p (j c)", j=4),
                    )
            if s >= 1:
                load_w2(wr, W2_AT, s - 1)
            if s >= 3 and s % 2 == 1:
                load_gate(wr, GATE_AT, (s - 3) // 2)
            if s == E:
                load_gate(wr, GATE_AT, E // 2 - 1)
            wraw[s] = wr

        grouped = {}

        def weights_pass(s, g):
            wr = wraw[s]
            if g == 0:
                gq = grpp.tile([P, PASSES, 4 * H], BF16, name="gq", align_bytes=64)
                w1c = w1cp.tile([P, PASSES, H], U32, name="w1c", align_bytes=64)
                w1s = w1cp.tile([P, PASSES, H], U8, name="w1s", align_bytes=64)
                grouped[s] = (gq, w1c, w1s)
            gq, w1c, w1s = grouped[s]
            last = s == E - 1
            dst = gq[:, g, :].rearrange("p (t m j) -> p m j t", t=4, m=P, j=4)
            src = wr[:, 4 * H * g : 4 * H * (g + 1)].rearrange("p (j m t) -> p m j t", j=4, t=4)
            if last and g == 0:
                cut = LAST_CUT
                nc.vector.tensor_copy(out=dst[:, 0:cut], in_=src[:, 0:cut])
                nc.scalar.copy(out=dst[:, cut:P], in_=src[:, cut:P])
            elif last:
                nc.vector.quantize_mx(
                    out=w1c[:, 0, :].bitcast(FP8X4), scales=w1s[:, 0, :], in_=gq[:, 0, :]
                )
                nc.vector.tensor_copy(out=dst[:, :, :, 0:2], in_=src[:, :, :, 0:2])
                nc.scalar.copy(out=dst[:, :, :, 2:4], in_=src[:, :, :, 2:4])
                for half in range(2):
                    nc.vector.quantize_mx(
                        out=w1c[:, 1, 2 * P * half : 2 * P * (half + 1)].bitcast(FP8X4),
                        scales=w1s[:, 1, 2 * P * half : 2 * P * (half + 1)],
                        in_=gq[:, 1, 2 * H * half : 2 * H * (half + 1)],
                    )
            elif g == 0:
                nc.scalar.copy(out=dst[:, 0:PASS0_CUT], in_=src[:, 0:PASS0_CUT])
            else:
                dst0 = gq[:, 0, :].rearrange("p (t m j) -> p m j t", t=4, m=P, j=4)
                src0 = wr[:, 0 : 4 * H].rearrange("p (j m t) -> p m j t", j=4, t=4)
                nc.vector.tensor_copy(out=dst0[:, PASS0_CUT:P], in_=src0[:, PASS0_CUT:P])
                nc.vector.tensor_copy(out=dst, in_=src)
            if g == 0:
                return
            if not last:
                nc.vector.quantize_mx(
                    out=w1c[:].rearrange("p g c -> p (g c)").bitcast(FP8X4),
                    scales=w1s[:].rearrange("p g c -> p (g c)"),
                    in_=gq[:].rearrange("p g c -> p (g c)"),
                )
            codes[s] = (w1c, w1s)

        load_step(0)

        x_view = xT.rearrange("(g p u e) n -> g u p (e n)", g=PASSES, p=P, u=2, e=2)
        xraw = {}
        for g in range(PASSES):
            for u in range(2):
                xr = rawp.tile([P, RAW_COLS], F32, name="raw")
                nc.sync.dma_start(out=xr[:, 0 : 2 * T], in_=x_view[g, u])
                xraw[(g, u)] = xr

        codes = {}
        weights_pass(0, 0)
        weights_pass(0, 1)

        pairs = {}
        for g in range(PASSES):
            for u in range(2):
                pt = keep.tile([P, T, 2], BF16, name="pairs%d%d" % (g, u))
                xr = xraw[(g, u)][:, 0 : 2 * T].rearrange("p (e n) -> p e n", e=2)
                nc.scalar.copy(
                    out=pt[:, 0:S_TOK, :].rearrange("p (c i) e -> p c e i", i=4),
                    in_=xr[:, :, 0:S_TOK].rearrange("p e (c i) -> p c e i", i=4),
                )
                nc.gpsimd.tensor_scalar(
                    out=pt[:, S_TOK:T, :],
                    in0=xr[:, :, S_TOK:T].rearrange("p e n -> p n e"),
                    scalar1=1.0,
                    scalar2=0.0,
                    op0=MULT,
                    op1=ADD,
                )
                pairs[(g, u)] = pt

        for s in range(1, AHEAD + 1):
            load_step(s)

        xc = {}
        xs = {}

        def tokens(g):
            xg = keep.tile([P, E * C, 4], BF16, name="xg%d" % g, align_bytes=64)
            words = xg[:].rearrange("p n t -> p (n t)").bitcast(U32)
            words = words.rearrange("p (n u) -> p n u", u=2)
            for u in range(2):
                win = pairs[(g, u)][:].rearrange("p n e -> p (n e)").bitcast(U32)
                nc.vector.tensor_copy(out=words[:, :, u], in_=win.indirect(offs_t[:]))
            xcg = keep.tile([P, E * C], U32, name="xc%d" % g, align_bytes=64)
            xsg = keep.tile([P, E * C], U8, name="xs%d" % g, align_bytes=64)
            nc.vector.quantize_mx(
                out=xcg[:].bitcast(FP8X4),
                scales=xsg[:],
                in_=xg[:].rearrange("p n t -> p (n t)"),
            )
            xc[g] = xcg
            xs[g] = xsg

        a_tiles = {}
        y_tiles = {}

        def layer1(s):
            w1c, w1s = codes[s]
            cols = slice(C * s, C * (s + 1))
            if s == E - 1:
                banks = [lps.tile([P, 2, C], F32, name="a_half") for half in range(2)]
            else:
                a_ps = aps.tile([P, 4, C], F32, name="a_ps")
                banks = [a_ps[:, 0:2, :], a_ps[:, 2:4, :]]
            for t in range(4):
                for g in range(PASSES):
                    nc.tensor.matmul_mx(
                        out=banks[t // 2][:, t % 2, :],
                        lhsT=w1c[:, g, P * t : P * (t + 1)].bitcast(FP8X4),
                        lhsT_scale=w1s[:, g, P * t : P * (t + 1)],
                        rhs=xc[g][:, cols].bitcast(FP8X4),
                        rhs_scale=xs[g][:, cols],
                        start=(g == 0),
                        stop=(g == PASSES - 1),
                    )
            a_tiles[s] = banks if s == E - 1 else a_ps

        def layer2(e):
            hw = hp.tile([P, 2 * 4 * C], BF16, name="hw", align_bytes=64)
            h_view = hw[:, 0 : 4 * C].rearrange("p (c t) -> p c t", t=4)
            if e == E - 1:
                for half in range(2):
                    nc.scalar.activation(
                        out=h_view[:, :, 2 * half : 2 * half + 2],
                        in_=a_tiles[e][half][:].rearrange("p t c -> p c t"),
                        func=RELU,
                    )
            else:
                nc.scalar.activation(
                    out=h_view,
                    in_=a_tiles[e][:].rearrange("p t c -> p c t"),
                    func=RELU,
                )
            nc.scalar.copy(
                out=hw[:, 4 * C : 8 * C].rearrange("p (c i j) -> p c j i", i=4, j=4),
                in_=wraw[e + 1][:, W2_AT : W2_AT + 4 * N].rearrange("p (j c i) -> p c j i", j=4, i=4),
            )
            hwc = hp.tile([P, 2 * C], U32, name="hwc", align_bytes=64)
            hws = hp.tile([P, 2 * C], U8, name="hws", align_bytes=64)
            nc.vector.quantize_mx(out=hwc[:].bitcast(FP8X4), scales=hws[:], in_=hw[:])
            if e % 2 == 0:
                y_ps = yps.tile([P, 2, C], F32, name="y_ps")
                y_tiles[e // 2] = y_ps
            nc.tensor.matmul_mx(
                out=y_tiles[e // 2][:, e % 2, :],
                lhsT=hwc[:, C : 2 * C].bitcast(FP8X4),
                lhsT_scale=hws[:, C : 2 * C],
                rhs=hwc[:, 0:C].bitcast(FP8X4),
                rhs_scale=hws[:, 0:C],
                start=True,
                stop=True,
            )

        def way_back(pr, gate_tile):
            y_sb = yp.tile([P, 2 * C], F32, name="y_sb")
            nc.vector.tensor_tensor(
                out=y_sb[:],
                in0=y_tiles[pr][:].rearrange("p e c -> p (e c)"),
                in1=gate_tile[:, GATE_AT : GATE_AT + 2 * C],
                op=MULT,
            )
            nc.vector.tensor_copy(
                out=window[:].indirect(offs_t[:, 16 * pr : 16 * (pr + 1)]),
                in_=y_sb[:],
            )

        weights_pass(1, 0)
        tokens(0)
        tokens(1)
        for s in range(E + 1):
            if s + 2 <= E - 1:
                weights_pass(s + 2, 0)
            if 1 <= s < E:
                weights_pass(s, 1)
            if s < E:
                layer1(s)
            if s >= 1:
                layer2(s - 1)
            if s >= 3 and s % 2 == 1:
                way_back((s - 3) // 2, wraw[s])
            if s == E:
                way_back(E // 2 - 1, wraw[s])
            if s >= 1 and s + AHEAD <= E:
                load_step(s + AHEAD)

        nc.sync.dma_start(out=out, in_=window[:])
